import numpy as np
import ml_dtypes


def mxq(x, axis, fmt="e4m3"):
    dtype, down = {"e4m3": (ml_dtypes.float8_e4m3fn, 7), "e5m2": (ml_dtypes.float8_e5m2, 14)}[fmt]
    v = np.moveaxis(np.asarray(x, np.float32).astype(ml_dtypes.bfloat16).astype(np.float64), axis, -1)
    blocks = v.reshape(v.shape[:-1] + (-1, 32))
    amax = np.abs(blocks).max(-1, keepdims=True)
    byte = np.maximum(np.where(amax > 0, np.frexp(amax)[1] - 1 + 127, 0) - down, 1)
    scale = np.exp2(byte - 127.0)
    codes = (blocks / scale).astype(np.float32).astype(dtype).astype(np.float64)
    return np.moveaxis((codes * scale).reshape(v.shape), -1, axis)


WIDE = False


def mx_kscale(k):
    if not WIDE:
        return np.ones(k)
    levels = np.array([30, -30])
    if k % 512:
        return np.exp2(np.random.permutation(np.resize(levels, k // 32))).repeat(32)
    a = np.empty((k // 512, 16))
    for p in range(k // 512):
        a[p, :8] = np.random.permutation(np.resize(levels, 8))
        for g in range(8):
            far = levels[np.abs(levels - a[p, g]) >= 10]
            a[p, g + 8] = far[np.random.randint(len(far))]
    return np.exp2(a.ravel()).repeat(32)


def f64(x):
    return np.asarray(x).astype(np.float64)


def striped(idx):
    return np.tile(np.asarray(idx).reshape(-1, 16).T, (8, 1)).astype(np.uint16)


def unstriped(offs):
    return offs[:16].T.reshape(-1).astype(np.int64)


E2M1 = np.array([0.0, 0.5, 1.0, 1.5, 2.0, 3.0, 4.0, 6.0, -0.0, -0.5, -1.0, -1.5, -2.0, -3.0, -4.0, -6.0])


def pack_weight(w, fmt):
    k, n = w.shape
    w = f64(np.asarray(w, np.float32).astype(ml_dtypes.bfloat16)).reshape(k // 32, 32, n)
    amax = np.abs(w).max(1)
    if fmt in ("e4m3", "e5m2"):
        byte = np.frexp(amax)[1] - 1 + 127 - (7 if fmt == "e4m3" else 14)
    else:
        mant, ex = np.frexp(amax / 6.0)
        byte = np.where(mant > 0.5, ex, ex - 1) + 127
    byte = np.clip(np.where(amax > 0, byte, 1), 1, 254)
    scaled = (w * np.exp2(127.0 - byte)[:, None, :]).reshape(k, n).astype(np.float32)
    by_word = np.ascontiguousarray(scaled.reshape(k // 512, 128, 4, n).transpose(0, 1, 3, 2))
    if fmt in ("e4m3", "e5m2"):
        words = by_word.astype(ml_dtypes.float8_e4m3fn if fmt == "e4m3" else ml_dtypes.float8_e5m2).view(np.uint8)
    else:
        c = by_word.astype(ml_dtypes.float4_e2m1fn).view(np.uint8) & 0xF
        words = (c[..., 0::2] | (c[..., 1::2] << 4)).reshape(k // 512, 128, 2 * n)
    return np.ascontiguousarray(words), np.ascontiguousarray(byte.astype(np.uint8).reshape(k // 512, 16, n))


def unpack_weight(words, scales, fmt):
    g, _, n = scales.shape
    words = np.ascontiguousarray(words).reshape(g, 128, n, -1)
    if fmt in ("e4m3", "e5m2"):
        vals = words.view(ml_dtypes.float8_e4m3fn if fmt == "e4m3" else ml_dtypes.float8_e5m2).astype(np.float64)
    else:
        nib = np.empty((g, 128, n, 4), np.uint8)
        nib[..., 0::2] = words & 0xF
        nib[..., 1::2] = words >> 4
        vals = E2M1[nib]
    vals = vals * np.repeat(np.exp2(scales.astype(np.float64) - 127.0), 8, axis=1)[..., None]
    return vals.transpose(0, 1, 3, 2).reshape(g * 512, n)


def sigmoid(v):
    return 1.0 / (1.0 + np.exp(-v))


K, T, J, R, O, N, E = 512, 2048, 256, 512, 128, 256, 512


def setup_inputs():
    n = np.random.standard_normal
    idx = np.random.permutation(T)[:J]
    idx2 = np.random.permutation(T)[:J]
    idx3 = np.random.permutation(T)[:J]
    idx4 = np.random.permutation(J)[:O]
    idx5 = np.random.permutation(J)[:O]
    idx6 = np.random.permutation(E)[:O]
    fk = mx_kscale(K)
    fr = mx_kscale(R)
    xtp = pack_weight(n((K, T)) / fk[:, None], "e2m1")
    wp = pack_weight(n((K, R)) * 1 / np.sqrt(K) * fk[:, None] * fr, "e5m2")
    wbp = pack_weight(n((R, N)) * 1 / np.sqrt(R) / fr[:, None], "e4m3")
    return {
        "xt_words": xtp[0],
        "xt_scales": xtp[1],
        "w_words": wp[0],
        "w_scales": wp[1],
        "wb_words": wbp[0],
        "wb_scales": wbp[1],
        "tz": (n((N, E))).astype(np.float32),
        "so": (np.random.uniform(0.6, 1.6, (N, 1))).astype(np.float32),
        "bo": (np.random.uniform(-1.0, 1.0, (N, 1))).astype(np.float32),
        "offs": striped(idx),
        "offs2": striped(idx2),
        "offs3": striped(idx3),
        "offs4": striped(idx4),
        "offs5": striped(idx5),
        "offs6": striped(idx6),
    }


def reference(xt_words, xt_scales, w_words, w_scales, wb_words, wb_scales, tz, so, bo, offs, offs2, offs3, offs4, offs5, offs6):
    idx = unstriped(offs)
    idx2 = unstriped(offs2)
    idx3 = unstriped(offs3)
    idx4 = unstriped(offs4)
    idx5 = unstriped(offs5)
    idx6 = unstriped(offs6)
    xtu = unpack_weight(xt_words, xt_scales, "e2m1")
    wu = unpack_weight(w_words, w_scales, "e5m2")
    wbu = unpack_weight(wb_words, wb_scales, "e4m3")
    xtidxg = xtu[:, idx]
    a = wu.T @ xtidxg
    xtidx2g = xtu[:, idx2]
    b = wu.T @ xtidx2g
    xtidx3g = xtu[:, idx3]
    g0 = wu.T @ xtidx3g
    c1 = np.maximum(b, g0)
    hid = np.abs(a[:, idx4] - c1[:, idx5])
    hidq = mxq(hid, 0, "e5m2")
    p = wbu.T @ hidq
    y = p * sigmoid(f64(tz)[:, idx6] * f64(so) + f64(bo))
    return y

@@ -1,0 +1,167 @@
+from contextlib import ExitStack
+
+import concourse.mybir as mybir
+
+K, T, J, R, O, N, E = 512, 2048, 256, 512, 128, 256, 512
+FLOPS = 2 * K * R * 3 * J + 2 * R * N * O
+
+F32 = mybir.dt.float32
+BF16 = mybir.dt.bfloat16
+I32 = mybir.dt.int32
+U32 = mybir.dt.uint32
+U16 = mybir.dt.uint16
+U8 = mybir.dt.uint8
+E2M1 = mybir.dt.float4_e2m1fn_x4
+E4M3 = mybir.dt.float8_e4m3fn_x4
+E5M2 = mybir.dt.float8_e5m2_x4
+ACT = mybir.ActivationFunctionType
+ALU = mybir.AluOpType
+
+P = 128
+PACK = 4
+HALVES = N // P
+SPLIT = O // 2
+
+
+def tile_list_triple_looked_one_finalgate_kernel(
+    tc, xt_words, xt_scales, w_words, w_scales, wb_words, wb_scales, tz, so, bo,
+    offs, offs2, offs3, offs4, offs5, offs6, out,
+):
+    nc = tc.nc
+    with ExitStack() as ctx:
+        sb = ctx.enter_context(tc.tile_pool(name="sb", bufs=1))
+        ps = ctx.enter_context(tc.psum_pool(name="ps", bufs=1))
+
+        def load_list(name, src):
+            lst = sb.tile(list(src.shape), U16, name=name)
+            nc.sync.dma_start(lst[:], src)
+            return lst
+
+        def zeroed_plane(name, width, eng):
+            plane = sb.tile([P, width], U8, name=name, align_bytes=64)
+            eng.memset(plane[:].bitcast(I32), 0)
+            return plane
+
+        def load_plane(plane, src, queues):
+            for r, queue in enumerate(queues):
+                queue.dma_start(plane[:].bitcast(I32)[r:P:32, :], src[0].bitcast(I32)[r:16:4, :])
+
+        xs = zeroed_plane("xs", T, nc.vector)
+        ws_raw = zeroed_plane("ws_raw", R, nc.gpsimd)
+        wbs = zeroed_plane("wbs", N, nc.vector)
+
+        ww_raw = sb.tile([P, R], U32, name="ww_raw")
+        nc.scalar.dma_start(ww_raw[:].bitcast(I32), w_words[0].rearrange("p c i -> p (c i)").bitcast(I32))
+        list_b = load_list("list_b", offs2)
+        list_a = load_list("list_a", offs)
+        load_plane(xs, xt_scales, [nc.scalar, nc.scalar, nc.sync, nc.sync])
+        xw = sb.tile([P, T], U16, name="xw")
+        nc.sync.dma_start(xw[:].bitcast(I32), xt_words[0].bitcast(I32))
+        load_plane(ws_raw, w_scales, [nc.gpsimd, nc.sync, nc.sync, nc.sync])
+        list_g = load_list("list_g", offs3)
+        pick_a = load_list("pick_a", offs4)
+        so_sb = sb.tile([P, HALVES], F32, name="so_sb")
+        bo_sb = sb.tile([P, HALVES], F32, name="bo_sb")
+        with nc.allow_non_contiguous_dma(reason="one value a partition and half"):
+            nc.sync.dma_start(so_sb[:], so.rearrange("(h p) one -> p (h one)", p=P))
+            nc.sync.dma_start(bo_sb[:], bo.rearrange("(h p) one -> p (h one)", p=P))
+        pick_z = load_list("pick_z", offs6)
+        tzs = []
+        for h in range(HALVES):
+            tzh = sb.tile([P, E], F32, name="tz%d" % h)
+            nc.sync.dma_start(tzh[:], tz[h * P:(h + 1) * P, :])
+            tzs.append(tzh)
+        pick_c = load_list("pick_c", offs5)
+        wbw = sb.tile([P, N], U32, name="wbw", align_bytes=64)
+        nc.sync.dma_start(wbw[:].bitcast(I32), wb_words[0].rearrange("p c i -> p (c i)").bitcast(I32))
+        load_plane(wbs, wb_scales, [nc.sync] * 4)
+
+        ww, ws = [], []
+        for u in range(2):
+            words = sb.tile([P, 2, P], U32, name="ww%d" % u, align_bytes=64)
+            nc.scalar.copy(
+                out=words[:].rearrange("p t (c i) -> p c t i", i=4),
+                in_=ww_raw[:].rearrange("p (c i t) -> p c t i", t=PACK, i=4)[:, :, 2 * u:2 * u + 2, :],
+            )
+            ww.append(words)
+            scales = sb.tile([P, 2, P], U8, name="ws%d" % u, align_bytes=64)
+            nc.gpsimd.tensor_copy(
+                out=scales[:].rearrange("p t (c i) -> p c t i", i=16),
+                in_=ws_raw[:].rearrange("p (c i t) -> p c t i", t=PACK, i=16)[:, :, 2 * u:2 * u + 2, :],
+            )
+            ws.append(scales)
+
+        def pick_tokens(name, lst):
+            scales = sb.tile([P, J], U8, name=name + "_s", align_bytes=64)
+            words = sb.tile([P, J], U16, name=name + "_w", align_bytes=64)
+            nc.vector.tensor_copy(out=scales[:], in_=xs[:].indirect(lst[:]))
+            nc.vector.tensor_copy(out=words[:], in_=xw[:].indirect(lst[:]))
+            return words, scales
+
+        def first_product(acc, picked, t):
+            words, scales = picked
+            nc.tensor.matmul_mx(
+                out=acc, lhsT=ww[t // 2][:, t % 2, :].bitcast(E5M2), lhsT_scale=ws[t // 2][:, t % 2, :],
+                rhs=words[:].bitcast(E2M1), rhs_scale=scales[:], start=True, stop=True,
+            )
+
+        def product_to_sbuf(name, picked):
+            pairs = []
+            for u in range(2):
+                bank = ps.tile([P, 2, J], F32, name="%s_bank%d" % (name, u))
+                for v in range(2):
+                    first_product(bank[:, v, :], picked, 2 * u + v)
+                pair = sb.tile([P, 2, J], F32, name="%s_sb%d" % (name, u))
+                nc.scalar.copy(out=pair[:], in_=bank[:])
+                pairs.append(pair)
+            return pairs
+
+        picked_b = pick_tokens("xb", list_b)
+        picked_a = pick_tokens("xa", list_a)
+        picked_g = pick_tokens("xg", list_g)
+
+        b_sb = product_to_sbuf("b", picked_b)
+        a_sb = product_to_sbuf("a", picked_a)
+        a_pick = sb.tile([P, PACK, O], F32, name="a_pick")
+        for t in range(PACK):
+            nc.scalar.activation(out=a_pick[:, t, :], in_=a_sb[t // 2][:, t % 2, :].indirect(pick_a[:]), func=ACT.Copy)
+
+        diff = sb.tile([P, PACK, O], F32, name="diff")
+        c1 = []
+        for t in range(PACK):
+            g_bank = ps.tile([P, J], F32, name="g_bank%d" % t)
+            first_product(g_bank[:], picked_g, t)
+            c1t = sb.tile([P, J], F32, name="c1_%d" % t)
+            nc.vector.tensor_tensor(out=c1t[:], in0=g_bank[:], in1=b_sb[t // 2][:, t % 2, :], op=ALU.max)
+            c1.append(c1t)
+        for t in range(PACK):
+            nc.vector.tensor_tensor(out=diff[:, t, :], in0=c1[t][:].indirect(pick_c[:]), in1=a_pick[:, t, :], op=ALU.subtract)
+
+        gate = sb.tile([P, HALVES, O], F32, name="gate")
+        for h in range(HALVES):
+            nc.scalar.activation(
+                out=gate[:, h, :], in_=tzs[h][:].indirect(pick_z[:]), func=ACT.Sigmoid,
+                bias=bo_sb[:, h:h + 1], scale=so_sb[:, h:h + 1],
+            )
+
+        hid = sb.tile([P, O, PACK], BF16, name="hid", align_bytes=64)
+        nc.scalar.activation(
+            out=hid[:, :SPLIT, :].rearrange("p (c i) t -> p c t i", i=4),
+            in_=diff[:, :, :SPLIT].rearrange("p t (c i) -> p c t i", i=4), func=ACT.Abs,
+        )
+        rest = diff[:, :, SPLIT:].rearrange("p t o -> p o t")
+        nc.vector.scalar_tensor_tensor(out=hid[:, SPLIT:, :], in0=rest, scalar=-1.0, in1=rest, op0=ALU.mult, op1=ALU.max)
+        hid_w = sb.tile([P, O], U32, name="hid_w", align_bytes=64)
+        hid_s = sb.tile([P, O], U8, name="hid_s", align_bytes=64)
+        nc.vector.quantize_mx(out=hid_w[:].bitcast(E5M2), scales=hid_s[:], in_=hid[:].rearrange("p o t -> p (o t)"))
+
+        for h, queue in enumerate([nc.sync, nc.scalar]):
+            cols = slice(h * P, (h + 1) * P)
+            p_bank = ps.tile([P, O], F32, name="p_bank%d" % h, tag="b_bank%d" % h)
+            nc.tensor.matmul_mx(
+                out=p_bank[:], lhsT=wbw[:, cols].bitcast(E4M3), lhsT_scale=wbs[:, cols],
+                rhs=hid_w[:].bitcast(E5M2), rhs_scale=hid_s[:], start=True, stop=True,
+            )
+            res = sb.tile([P, O], F32, name="res%d" % h)
+            nc.vector.tensor_tensor(out=res[:], in0=p_bank[:], in1=gate[:, h, :], op=ALU.mult)
+            queue.dma_start(out[cols, :], res[:])

@@ -76,6 +76,10 @@ def tile_list_triple_looked_one_finalgate_kernel(
         nc.sync.dma_start(wbw[:].bitcast(I32), wb_words[0].rearrange("p c i -> p (c i)").bitcast(I32))
         load_plane(wbs, wb_scales, [nc.sync] * 4)
 
+        warm = sb.tile([P, 2], F32, name="warm")
+        nc.vector.memset(warm[:, 0:1], 0.0)
+        nc.scalar.activation(out=warm[:, 1:2], in_=warm[:, 0:1], func=ACT.Sigmoid)
+
         ww, ws = [], []
         for u in range(2):
             words = sb.tile([P, 2, P], U32, name="ww%d" % u, align_bytes=64)

@@ -20,7 +20,7 @@ ALU = mybir.AluOpType
 P = 128
 PACK = 4
 HALVES = N // P
-SPLIT = O // 2
+SPLIT = 96
 
 
 def tile_list_triple_looked_one_finalgate_kernel(

@@ -83,7 +83,7 @@ def tile_list_triple_looked_one_finalgate_kernel(
         ww, ws = [], []
         for u in range(2):
             words = sb.tile([P, 2, P], U32, name="ww%d" % u, align_bytes=64)
-            nc.scalar.copy(
+            nc.gpsimd.tensor_copy(
                 out=words[:].rearrange("p t (c i) -> p c t i", i=4),
                 in_=ww_raw[:].rearrange("p (c i t) -> p c t i", t=PACK, i=4)[:, :, 2 * u:2 * u + 2, :],
             )

from contextlib import ExitStack

import concourse.mybir as mybir

K, T, J, R, O, N, E = 512, 2048, 256, 512, 128, 256, 512
FLOPS = 2 * K * R * 3 * J + 2 * R * N * O

F32 = mybir.dt.float32
BF16 = mybir.dt.bfloat16
I32 = mybir.dt.int32
U32 = mybir.dt.uint32
U16 = mybir.dt.uint16
U8 = mybir.dt.uint8
E2M1 = mybir.dt.float4_e2m1fn_x4
E4M3 = mybir.dt.float8_e4m3fn_x4
E5M2 = mybir.dt.float8_e5m2_x4
ACT = mybir.ActivationFunctionType
ALU = mybir.AluOpType

P = 128
PACK = 4
HALVES = N // P
SPLIT = 96


def tile_list_triple_looked_one_finalgate_kernel(
    tc, xt_words, xt_scales, w_words, w_scales, wb_words, wb_scales, tz, so, bo,
    offs, offs2, offs3, offs4, offs5, offs6, out,
):
    nc = tc.nc
    with ExitStack() as ctx:
        sb = ctx.enter_context(tc.tile_pool(name="sb", bufs=1))
        ps = ctx.enter_context(tc.psum_pool(name="ps", bufs=1))

        def load_list(name, src):
            lst = sb.tile(list(src.shape), U16, name=name)
            nc.sync.dma_start(lst[:], src)
            return lst

        def zeroed_plane(name, width, eng):
            plane = sb.tile([P, width], U8, name=name, align_bytes=64)
            eng.memset(plane[:].bitcast(I32), 0)
            return plane

        def load_plane(plane, src, queues):
            for r, queue in enumerate(queues):
                queue.dma_start(plane[:].bitcast(I32)[r:P:32, :], src[0].bitcast(I32)[r:16:4, :])

        xs = zeroed_plane("xs", T, nc.vector)
        ws_raw = zeroed_plane("ws_raw", R, nc.gpsimd)
        wbs = zeroed_plane("wbs", N, nc.vector)

        ww_raw = sb.tile([P, R], U32, name="ww_raw")
        nc.scalar.dma_start(ww_raw[:].bitcast(I32), w_words[0].rearrange("p c i -> p (c i)").bitcast(I32))
        list_b = load_list("list_b", offs2)
        list_a = load_list("list_a", offs)
        load_plane(xs, xt_scales, [nc.scalar, nc.scalar, nc.sync, nc.sync])
        xw = sb.tile([P, T], U16, name="xw")
        nc.sync.dma_start(xw[:].bitcast(I32), xt_words[0].bitcast(I32))
        load_plane(ws_raw, w_scales, [nc.gpsimd, nc.sync, nc.sync, nc.sync])
        list_g = load_list("list_g", offs3)
        pick_a = load_list("pick_a", offs4)
        so_sb = sb.tile([P, HALVES], F32, name="so_sb")
        bo_sb = sb.tile([P, HALVES], F32, name="bo_sb")
        with nc.allow_non_contiguous_dma(reason="one value a partition and half"):
            nc.sync.dma_start(so_sb[:], so.rearrange("(h p) one -> p (h one)", p=P))
            nc.sync.dma_start(bo_sb[:], bo.rearrange("(h p) one -> p (h one)", p=P))
        pick_z = load_list("pick_z", offs6)
        tzs = []
        for h in range(HALVES):
            tzh = sb.tile([P, E], F32, name="tz%d" % h)
            nc.sync.dma_start(tzh[:], tz[h * P:(h + 1) * P, :])
            tzs.append(tzh)
        pick_c = load_list("pick_c", offs5)
        wbw = sb.tile([P, N], U32, name="wbw", align_bytes=64)
        nc.sync.dma_start(wbw[:].bitcast(I32), wb_words[0].rearrange("p c i -> p (c i)").bitcast(I32))
        load_plane(wbs, wb_scales, [nc.sync] * 4)

        warm = sb.tile([P, 2], F32, name="warm")
        nc.vector.memset(warm[:, 0:1], 0.0)
        nc.scalar.activation(out=warm[:, 1:2], in_=warm[:, 0:1], func=ACT.Sigmoid)

        ww, ws = [], []
        for u in range(2):
            words = sb.tile([P, 2, P], U32, name="ww%d" % u, align_bytes=64)
            nc.gpsimd.tensor_copy(
                out=words[:].rearrange("p t (c i) -> p c t i", i=4),
                in_=ww_raw[:].rearrange("p (c i t) -> p c t i", t=PACK, i=4)[:, :, 2 * u:2 * u + 2, :],
            )
            ww.append(words)
            scales = sb.tile([P, 2, P], U8, name="ws%d" % u, align_bytes=64)
            nc.gpsimd.tensor_copy(
                out=scales[:].rearrange("p t (c i) -> p c t i", i=16),
                in_=ws_raw[:].rearrange("p (c i t) -> p c t i", t=PACK, i=16)[:, :, 2 * u:2 * u + 2, :],
            )
            ws.append(scales)

        def pick_tokens(name, lst):
            scales = sb.tile([P, J], U8, name=name + "_s", align_bytes=64)
            words = sb.tile([P, J], U16, name=name + "_w", align_bytes=64)
            nc.vector.tensor_copy(out=scales[:], in_=xs[:].indirect(lst[:]))
            nc.vector.tensor_copy(out=words[:], in_=xw[:].indirect(lst[:]))
            return words, scales

        def first_product(acc, picked, t):
            words, scales = picked
            nc.tensor.matmul_mx(
                out=acc, lhsT=ww[t // 2][:, t % 2, :].bitcast(E5M2), lhsT_scale=ws[t // 2][:, t % 2, :],
                rhs=words[:].bitcast(E2M1), rhs_scale=scales[:], start=True, stop=True,
            )

        def product_to_sbuf(name, picked):
            pairs = []
            for u in range(2):
                bank = ps.tile([P, 2, J], F32, name="%s_bank%d" % (name, u))
                for v in range(2):
                    first_product(bank[:, v, :], picked, 2 * u + v)
                pair = sb.tile([P, 2, J], F32, name="%s_sb%d" % (name, u))
                nc.scalar.copy(out=pair[:], in_=bank[:])
                pairs.append(pair)
            return pairs

        picked_b = pick_tokens("xb", list_b)
        picked_a = pick_tokens("xa", list_a)
        picked_g = pick_tokens("xg", list_g)

        b_sb = product_to_sbuf("b", picked_b)
        a_sb = product_to_sbuf("a", picked_a)
        a_pick = sb.tile([P, PACK, O], F32, name="a_pick")
        for t in range(PACK):
            nc.scalar.activation(out=a_pick[:, t, :], in_=a_sb[t // 2][:, t % 2, :].indirect(pick_a[:]), func=ACT.Copy)

        diff = sb.tile([P, PACK, O], F32, name="diff")
        c1 = []
        for t in range(PACK):
            g_bank = ps.tile([P, J], F32, name="g_bank%d" % t)
            first_product(g_bank[:], picked_g, t)
            c1t = sb.tile([P, J], F32, name="c1_%d" % t)
            nc.vector.tensor_tensor(out=c1t[:], in0=g_bank[:], in1=b_sb[t // 2][:, t % 2, :], op=ALU.max)
            c1.append(c1t)
        for t in range(PACK):
            nc.vector.tensor_tensor(out=diff[:, t, :], in0=c1[t][:].indirect(pick_c[:]), in1=a_pick[:, t, :], op=ALU.subtract)

        gate = sb.tile([P, HALVES, O], F32, name="gate")
        for h in range(HALVES):
            nc.scalar.activation(
                out=gate[:, h, :], in_=tzs[h][:].indirect(pick_z[:]), func=ACT.Sigmoid,
                bias=bo_sb[:, h:h + 1], scale=so_sb[:, h:h + 1],
            )

        hid = sb.tile([P, O, PACK], BF16, name="hid", align_bytes=64)
        nc.scalar.activation(
            out=hid[:, :SPLIT, :].rearrange("p (c i) t -> p c t i", i=4),
            in_=diff[:, :, :SPLIT].rearrange("p t (c i) -> p c t i", i=4), func=ACT.Abs,
        )
        rest = diff[:, :, SPLIT:].rearrange("p t o -> p o t")
        nc.vector.scalar_tensor_tensor(out=hid[:, SPLIT:, :], in0=rest, scalar=-1.0, in1=rest, op0=ALU.mult, op1=ALU.max)
        hid_w = sb.tile([P, O], U32, name="hid_w", align_bytes=64)
        hid_s = sb.tile([P, O], U8, name="hid_s", align_bytes=64)
        nc.vector.quantize_mx(out=hid_w[:].bitcast(E5M2), scales=hid_s[:], in_=hid[:].rearrange("p o t -> p (o t)"))

        for h, queue in enumerate([nc.sync, nc.scalar]):
            cols = slice(h * P, (h + 1) * P)
            p_bank = ps.tile([P, O], F32, name="p_bank%d" % h, tag="b_bank%d" % h)
            nc.tensor.matmul_mx(
                out=p_bank[:], lhsT=wbw[:, cols].bitcast(E4M3), lhsT_scale=wbs[:, cols],
                rhs=hid_w[:].bitcast(E5M2), rhs_scale=hid_s[:], start=True, stop=True,
            )
            res = sb.tile([P, O], F32, name="res%d" % h)
            nc.vector.tensor_tensor(out=res[:], in0=p_bank[:], in1=gate[:, h, :], op=ALU.mult)
            queue.dma_start(out[cols, :], res[:])
